import numpy as np
import ml_dtypes


def mxq(x, axis, fmt="e4m3"):
    dtype, down = {"e4m3": (ml_dtypes.float8_e4m3fn, 7), "e5m2": (ml_dtypes.float8_e5m2, 14)}[fmt]
    v = np.moveaxis(np.asarray(x, np.float32).astype(ml_dtypes.bfloat16).astype(np.float64), axis, -1)
    blocks = v.reshape(v.shape[:-1] + (-1, 32))
    amax = np.abs(blocks).max(-1, keepdims=True)
    byte = np.maximum(np.where(amax > 0, np.frexp(amax)[1] - 1 + 127, 0) - down, 1)
    scale = np.exp2(byte - 127.0)
    codes = (blocks / scale).astype(np.float32).astype(dtype).astype(np.float64)
    return np.moveaxis((codes * scale).reshape(v.shape), -1, axis)


WIDE = False


def mx_kscale(k):
    if not WIDE:
        return np.ones(k)
    levels = np.array([10, -10, 5, -5, 0])
    if k % 512:
        return np.exp2(np.random.permutation(np.resize(levels, k // 32))).repeat(32)
    a = np.empty((k // 512, 16))
    for p in range(k // 512):
        a[p, :8] = np.random.permutation(np.resize(levels, 8))
        for g in range(8):
            far = levels[np.abs(levels - a[p, g]) >= 10]
            a[p, g + 8] = far[np.random.randint(len(far))]
    return np.exp2(a.ravel()).repeat(32)


def f64(x):
    return np.asarray(x).astype(np.float64)


def striped(idx):
    return np.tile(np.asarray(idx).reshape(-1, 16).T, (8, 1)).astype(np.uint16)


def unstriped(offs):
    return offs[:16].T.reshape(-1).astype(np.int64)


E2M1 = np.array([0.0, 0.5, 1.0, 1.5, 2.0, 3.0, 4.0, 6.0, -0.0, -0.5, -1.0, -1.5, -2.0, -3.0, -4.0, -6.0])


def pack_weight(w, fmt):
    k, n = w.shape
    w = f64(np.asarray(w, np.float32).astype(ml_dtypes.bfloat16)).reshape(k // 32, 32, n)
    amax = np.abs(w).max(1)
    if fmt == "e4m3":
        byte = np.frexp(amax)[1] - 1 + 127 - 7
    else:
        mant, ex = np.frexp(amax / 6.0)
        byte = np.where(mant > 0.5, ex, ex - 1) + 127
    byte = np.clip(np.where(amax > 0, byte, 1), 1, 254)
    scaled = (w * np.exp2(127.0 - byte)[:, None, :]).reshape(k, n).astype(np.float32)
    by_word = np.ascontiguousarray(scaled.reshape(k // 512, 128, 4, n).transpose(0, 1, 3, 2))
    if fmt == "e4m3":
        words = by_word.astype(ml_dtypes.float8_e4m3fn).view(np.uint8)
    else:
        c = by_word.astype(ml_dtypes.float4_e2m1fn).view(np.uint8) & 0xF
        words = (c[..., 0::2] | (c[..., 1::2] << 4)).reshape(k // 512, 128, 2 * n)
    return np.ascontiguousarray(words), np.ascontiguousarray(byte.astype(np.uint8).reshape(k // 512, 16, n))


def unpack_weight(words, scales, fmt):
    g, _, n = scales.shape
    words = np.ascontiguousarray(words).reshape(g, 128, n, -1)
    if fmt == "e4m3":
        vals = words.view(ml_dtypes.float8_e4m3fn).astype(np.float64)
    else:
        nib = np.empty((g, 128, n, 4), np.uint8)
        nib[..., 0::2] = words & 0xF
        nib[..., 1::2] = words >> 4
        vals = E2M1[nib]
    vals = vals * np.repeat(np.exp2(scales.astype(np.float64) - 127.0), 8, axis=1)[..., None]
    return vals.transpose(0, 1, 3, 2).reshape(g * 512, n)


D, E, T, I, Q, G = 512, 512, 2048, 512, 256, 32


def setup_inputs():
    n = np.random.standard_normal
    idx = np.random.permutation(T)[:I]
    fd = mx_kscale(D)
    fe = mx_kscale(E)
    keysp = pack_weight(n((D, T)) / fd[:, None], "e2m1")
    valsp = pack_weight(n((E, T)) / fe[:, None], "e2m1")
    return {
        "query": (n((D, Q)) * 0.7 / np.sqrt(D) * fd[:, None]).astype(np.float32),
        "keys_words": keysp[0],
        "keys_scales": keysp[1],
        "reserve": (np.random.uniform(1.0, 8.0, (I, 1))).astype(np.float32),
        "us": (np.random.uniform(0.5, 2.0, (I, 1))).astype(np.float32),
        "gout": (n((E, Q)) * 1 / np.sqrt(E) * fe[:, None]).astype(np.float32),
        "vals_words": valsp[0],
        "vals_scales": valsp[1],
        "base": (0.5 * n((I, Q))).astype(np.float32),
        "offs": striped(idx),
    }


def reference(query, keys_words, keys_scales, reserve, us, gout, vals_words, vals_scales, base, offs):
    idx = unstriped(offs)
    keysu = unpack_weight(keys_words, keys_scales, "e2m1")
    valsu = unpack_weight(vals_words, vals_scales, "e2m1")
    keysidxg = keysu[:, idx]
    queryq = mxq(f64(query), 0, "e4m3")
    a = keysidxg.T @ queryq
    p = np.exp(a)
    b = f64(us) / (p.reshape(I, G, Q // G).sum(axis=2) + f64(reserve))
    br = np.repeat(b, Q // G, axis=1)
    valsidxg = valsu[:, idx]
    goutq = mxq(f64(gout), 0, "e4m3")
    c0 = valsidxg.T @ goutq
    dbr = c0 * p
    db = dbr.reshape(I, G, Q // G).sum(axis=2)
    e1 = db * f64(us) / np.square(p.reshape(I, G, Q // G).sum(axis=2) + f64(reserve)) * (-1.0)
    r1 = np.repeat(e1, Q // G, axis=1)
    dp = c0 * br + r1
    da = dp * p
    hda = da * 16.0 * 2.0 * 16.0
    hdp = hda * p
    he1 = hdp.reshape(I, G, Q // G).sum(axis=2)
    e51 = he1 * (-1.0) * db * f64(us) / np.square(np.square(p.reshape(I, G, Q // G).sum(axis=2) + f64(reserve))) * (-1.0) * (p.reshape(I, G, Q // G).sum(axis=2) + f64(reserve)) * 2.0
    r51 = np.repeat(e51, Q // G, axis=1)
    hdb = he1 * (-1.0) / np.square(p.reshape(I, G, Q // G).sum(axis=2) + f64(reserve)) * f64(us)
    r52 = np.repeat(hdb, Q // G, axis=1)
    hbr = hdp * c0
    hb = hbr.reshape(I, G, Q // G).sum(axis=2)
    e53 = hb * f64(us) / np.square(p.reshape(I, G, Q // G).sum(axis=2) + f64(reserve)) * (-1.0)
    r53 = np.repeat(e53, Q // G, axis=1)
    hp = hda * dp + r51 + r52 * c0 + r53
    ha = hp * p
    y = ha + f64(base)
    return y

@@ -1,0 +1,218 @@
+import math
+from contextlib import ExitStack
+
+import concourse.mybir as mybir
+from concourse.masks import make_identity
+
+F32 = mybir.dt.float32
+BF16 = mybir.dt.bfloat16
+I32 = mybir.dt.int32
+U32 = mybir.dt.uint32
+U16 = mybir.dt.uint16
+U8 = mybir.dt.uint8
+FP8X4 = mybir.dt.float8_e4m3fn_x4
+FP4X4 = mybir.dt.float4_e2m1fn_x4
+ALU = mybir.AluOpType
+ACT = mybir.ActivationFunctionType
+AXIS = mybir.AxisListType
+
+P = 128
+POOL = 2048
+SLOTS = 512
+ROWS = 256
+TEAMS = 32
+TILES = SLOTS // P
+PAIRS = 4
+PACK = 4
+FLOPS = 2 * 2 * 512 * SLOTS * ROWS
+
+
+def tile_attend_gpteamshares_kernel(tc, query, keys_words, keys_scales, reserve, us, gout, vals_words, vals_scales, base, offs, out):
+    nc = tc.nc
+    with ExitStack() as ctx:
+        keep = ctx.enter_context(tc.tile_pool(name="keep", bufs=1))
+        psum = ctx.enter_context(tc.psum_pool(name="psum", bufs=1))
+
+        def sb(name, shape, dtype, tag=None):
+            return keep.tile(shape, dtype, name=name, tag=tag or name, align_bytes=64)
+
+        def load_scales(queue, plane, scales):
+            for quad in range(4):
+                queue.dma_start(out=plane[32 * quad : 32 * quad + 4, :].bitcast(I32), in_=scales[0, 4 * quad : 4 * quad + 4, :].bitcast(I32))
+
+        def by_team(cols):
+            return cols.unsqueeze(1).unsqueeze(3).to_broadcast([P, PAIRS, TEAMS, 2])
+
+        def dealt(tile):
+            return tile.rearrange("p (a g b) -> p a g b", a=PAIRS, b=2)
+
+        def quantise(name, raw):
+            grouped = sb(name + "_bf", [P, ROWS * PACK], BF16)
+            codes = sb(name + "_codes", [P, ROWS], U32)
+            plane = sb(name + "_plane", [P, ROWS], U8)
+            nc.scalar.copy(
+                out=grouped[:].rearrange("p (a g b k) -> p g a k b", a=PAIRS, b=2, k=PACK),
+                in_=raw[:].rearrange("p k (g a b) -> p g a k b", a=PAIRS, b=2),
+            )
+            nc.vector.quantize_mx(out=codes[:].bitcast(FP8X4), scales=plane[:], in_=grouped[:])
+            return codes, plane
+
+        def products(names, words, plane, codes, code_plane):
+            banks = [psum.tile([P, 2, ROWS], F32, name=n, tag=n) for n in names]
+            for t in range(TILES):
+                cols = slice(t * P, (t + 1) * P)
+                nc.tensor.matmul_mx(
+                    out=banks[t // 2][:, t % 2, :],
+                    lhsT=words[:, cols].bitcast(FP4X4),
+                    lhsT_scale=plane[:, cols],
+                    rhs=codes[:].bitcast(FP8X4),
+                    rhs_scale=code_plane[:],
+                    start=True,
+                    stop=True,
+                )
+            return banks
+
+        offsets = keep.tile([P, SLOTS // 16], U16, name="offsets")
+        nc.sync.dma_start(offsets[:], offs)
+
+        key_plane = sb("key_plane", [P, POOL], U8)
+        val_plane = sb("val_plane", [P, POOL], U8)
+        nc.gpsimd.memset(key_plane[:].bitcast(I32), 0)
+        nc.vector.memset(val_plane[:].bitcast(I32), 0)
+
+        q_raw = sb("q_raw", [P, PACK, ROWS], F32)
+        key_words = sb("key_words", [P, POOL], U16)
+        val_words = sb("val_words", [P, POOL], U16)
+        us_sb = sb("us_sb", [P, TILES], F32)
+        res_sb = sb("res_sb", [P, TILES], F32)
+
+        nc.sync.dma_start(out=q_raw[:], in_=query.rearrange("(p k) q -> p k q", k=PACK))
+        load_scales(nc.sync, key_plane, keys_scales)
+        nc.sync.dma_start(out=key_words[:].bitcast(I32), in_=keys_words[0].bitcast(I32))
+        load_scales(nc.sync, val_plane, vals_scales)
+        nc.sync.dma_start(out=val_words[:].bitcast(I32), in_=vals_words[0].bitcast(I32))
+        with nc.allow_non_contiguous_dma(reason="one float32 for each slot"):
+            nc.gpsimd.dma_start(out=res_sb[:], in_=reserve.rearrange("(t p) o -> p (t o)", p=P))
+            nc.gpsimd.dma_start(out=us_sb[:], in_=us.rearrange("(t p) o -> p (t o)", p=P))
+
+        ident = sb("ident", [P, P], F32)
+        make_identity(nc, ident[:])
+        kappa = sb("kappa", [P, TILES], F32)
+        res_wide = sb("res_wide", [P, TILES, TEAMS], F32)
+
+        got_kplane = sb("got_kplane", [P, SLOTS], U8)
+        got_kwords = sb("got_kwords", [P, SLOTS], U16)
+        got_vplane = sb("got_vplane", [P, SLOTS], U8)
+        got_vwords = sb("got_vwords", [P, SLOTS], U16)
+
+        nc.vector.tensor_copy(got_kplane[:], key_plane[:].indirect(offsets[:]))
+        q_codes, q_plane = quantise("q", q_raw)
+        g_raw = sb("g_raw", [P, PACK, ROWS], F32, tag="q_raw")
+        nc.sync.dma_start(out=g_raw[:], in_=gout.rearrange("(p k) q -> p k q", k=PACK))
+        nc.scalar.mul(kappa[:], us_sb[:], math.sqrt(512.0))
+        nc.gpsimd.tensor_copy(out=res_wide[:], in_=res_sb[:].unsqueeze(2).to_broadcast([P, TILES, TEAMS]))
+        for h in range(2):
+            nc.vector.tensor_copy(got_kwords[:, h * 256 : (h + 1) * 256], key_words[:].indirect(offsets[:, h * 16 : (h + 1) * 16]))
+        base_sb = sb("base_sb", [P, TILES, ROWS], F32, tag="key_words")
+        nc.sync.dma_start(out=base_sb[:], in_=base.rearrange("(t p) q -> p t q", p=P))
+        a_banks = products(["bank0", "bank1"], got_kwords, got_kplane, q_codes, q_plane)
+
+        p_all = sb("p_all", [P, PAIRS, TILES * 2 * TEAMS], F32)
+        for t in range(TILES):
+            nc.scalar.activation(
+                out=p_all[:, :, t * 64 : (t + 1) * 64],
+                in_=a_banks[t // 2][:, t % 2, :].rearrange("p (a c) -> p a c", a=PAIRS),
+                func=ACT.Exp,
+            )
+
+        def team_sums(bank, src, first):
+            blocks = list(first) + [src[:, a, b : 2 * P : 2] for a in range(PAIRS) for b in range(2)]
+            for n, block in enumerate(blocks):
+                nc.tensor.matmul(bank[:], lhsT=block, rhs=ident[:], is_transpose=True, start=(n == 0), stop=(n == len(blocks) - 1))
+
+        sum_bank = psum.tile([P, P], F32, name="sum_bank", tag="bank4")
+        team_sums(sum_bank, p_all, [res_wide[:].rearrange("p t g -> p (t g)")])
+
+        nc.vector.tensor_copy(got_vplane[:], val_plane[:].indirect(offsets[:]))
+        nc.vector.tensor_copy(got_vwords[:], val_words[:].indirect(offsets[:]))
+        g_codes, g_plane = quantise("g", g_raw)
+        c_banks = products(["bank2", "bank3"], got_vwords, got_vplane, g_codes, g_plane)
+
+        inv_turned = sb("inv_turned", [P, P], F32)
+        nc.vector.reciprocal(inv_turned[:], sum_bank[:])
+        inv_bank = psum.tile([P, P], F32, name="inv_bank", tag="bank5")
+        nc.tensor.transpose(inv_bank[:], inv_turned[:], ident[:])
+
+        s = [sb("s%d" % t, [P, ROWS], F32) for t in range(TILES)]
+        cs = [sb("cs%d" % t, [P, ROWS], F32) for t in range(TILES)]
+        m = [sb("m%d" % t, [P, TEAMS], F32) for t in range(TILES)]
+        x = [sb("x%d" % t, [P, ROWS], F32) for t in range(TILES)]
+        z = [sb("z%d" % t, [P, ROWS], F32) for t in range(TILES)]
+        hw_banks = []
+        for h in range(2):
+            tiles = (2 * h, 2 * h + 1)
+            terms = sb("terms%d" % h, [P, PAIRS, 2 * P], F32)
+            for t in tiles:
+                nc.vector.tensor_tensor(
+                    out=dealt(s[t][:]),
+                    in0=p_all[:, :, t * 64 : (t + 1) * 64].rearrange("p a (g b) -> p a g b", b=2),
+                    in1=by_team(inv_bank[:, t * TEAMS : (t + 1) * TEAMS]),
+                    op=ALU.mult,
+                )
+            for t in tiles:
+                nc.vector.tensor_tensor(out=cs[t][:], in0=c_banks[h][:, t % 2, :], in1=s[t][:], op=ALU.mult)
+            for t in tiles:
+                nc.vector.tensor_reduce(
+                    out=m[t][:], in_=cs[t][:].rearrange("p (a g b) -> p g a b", a=PAIRS, b=2), axis=AXIS.XY, op=ALU.add
+                )
+            for t in tiles:
+                nc.vector.tensor_tensor(out=dealt(x[t][:]), in0=dealt(c_banks[h][:, t % 2, :]), in1=by_team(m[t][:]), op=ALU.subtract)
+            for t in tiles:
+                nc.vector.scalar_tensor_tensor(
+                    out=z[t][:], in0=x[t][:], scalar=kappa[:, t : t + 1], in1=s[t][:], op0=ALU.mult, op1=ALU.mult
+                )
+            for t in tiles:
+                at = (t % 2) * 64
+                nc.vector.tensor_tensor(
+                    out=terms[:, :, at : at + 64],
+                    in0=z[t][:].rearrange("p (a c) -> p a c", a=PAIRS),
+                    in1=s[t][:].rearrange("p (a c) -> p a c", a=PAIRS),
+                    op=ALU.mult,
+                )
+                nc.scalar.activation(
+                    out=terms[:, :, P + at : P + at + 64], in_=z[t][:].rearrange("p (a c) -> p a c", a=PAIRS), func=ACT.Square
+                )
+            turned_bank = psum.tile([P, P], F32, name="turned_bank%d" % h, tag=("bank6", "bank0")[h])
+            team_sums(turned_bank, terms, [])
+            turned = sb("turned%d" % h, [P, P], F32)
+            nc.scalar.copy(out=turned[:], in_=turned_bank[:])
+            hw_bank = psum.tile([P, P], F32, name="hw_bank%d" % h, tag=("bank7", "bank1")[h])
+            nc.tensor.transpose(hw_bank[:], turned[:], ident[:])
+            hw_banks.append(hw_bank)
+
+        out_tiles = out.rearrange("(t p) q -> t p q", p=P)
+        for h in range(2):
+            tiles = (2 * h, 2 * h + 1)
+            zh = {t: sb("zh%d" % t, [P, ROWS], F32) for t in tiles}
+            ws = {t: sb("ws%d" % t, [P, ROWS], F32) for t in tiles}
+            zzh = {t: sb("zzh%d" % t, [P, ROWS], F32) for t in tiles}
+            ha = {t: sb("ha%d" % t, [P, ROWS], F32) for t in tiles}
+            for t in tiles:
+                at = (t % 2) * TEAMS
+                nc.vector.tensor_tensor(out=dealt(zh[t][:]), in0=dealt(z[t][:]), in1=by_team(hw_banks[h][:, at : at + TEAMS]), op=ALU.subtract)
+            for t in tiles:
+                at = (2 + t % 2) * TEAMS
+                nc.vector.tensor_tensor(out=dealt(ws[t][:]), in0=dealt(s[t][:]), in1=by_team(hw_banks[h][:, at : at + TEAMS]), op=ALU.mult)
+            for t in tiles:
+                nc.vector.tensor_tensor(out=zzh[t][:], in0=zh[t][:], in1=z[t][:], op=ALU.mult)
+            for t in tiles:
+                nc.vector.tensor_tensor(out=ha[t][:], in0=zzh[t][:], in1=ws[t][:], op=ALU.subtract)
+            for t in tiles:
+                res = sb("res%d" % t, [P, ROWS], F32)
+                nc.vector.tensor_tensor(
+                    out=res[:].rearrange("p (g a b) -> p g a b", a=PAIRS, b=2),
+                    in0=ha[t][:].rearrange("p (a g b) -> p g a b", a=PAIRS, b=2),
+                    in1=base_sb[:, t, :].rearrange("p (g a b) -> p g a b", a=PAIRS, b=2),
+                    op=ALU.add,
+                )
+                nc.sync.dma_start(out=out_tiles[t], in_=res[:])

@@ -2,7 +2,6 @@ import math
 from contextlib import ExitStack
 
 import concourse.mybir as mybir
-from concourse.masks import make_identity
 
 F32 = mybir.dt.float32
 BF16 = mybir.dt.bfloat16
@@ -22,7 +21,7 @@ SLOTS = 512
 ROWS = 256
 TEAMS = 32
 TILES = SLOTS // P
-PAIRS = 4
+MATES = 8
 PACK = 4
 FLOPS = 2 * 2 * 512 * SLOTS * ROWS
 
@@ -31,188 +30,221 @@ def tile_attend_gpteamshares_kernel(tc, query, keys_words, keys_scales, reserve,
     nc = tc.nc
     with ExitStack() as ctx:
         keep = ctx.enter_context(tc.tile_pool(name="keep", bufs=1))
+        shared = ctx.enter_context(tc.tile_pool(name="shared", bufs=1))
         psum = ctx.enter_context(tc.psum_pool(name="psum", bufs=1))
 
         def sb(name, shape, dtype, tag=None):
             return keep.tile(shape, dtype, name=name, tag=tag or name, align_bytes=64)
 
         def load_scales(queue, plane, scales):
-            for quad in range(4):
-                queue.dma_start(out=plane[32 * quad : 32 * quad + 4, :].bitcast(I32), in_=scales[0, 4 * quad : 4 * quad + 4, :].bitcast(I32))
+            for r in range(4):
+                queue.dma_start(out=plane[r:P:32, :].bitcast(I32), in_=scales[0, r:16:4, :].bitcast(I32))
 
-        def by_team(cols):
-            return cols.unsqueeze(1).unsqueeze(3).to_broadcast([P, PAIRS, TEAMS, 2])
+        def by_team(cols, mates):
+            return cols.unsqueeze(1).to_broadcast([P, mates, cols.shape[1]])
 
-        def dealt(tile):
-            return tile.rearrange("p (a g b) -> p a g b", a=PAIRS, b=2)
-
-        def quantise(name, raw):
-            grouped = sb(name + "_bf", [P, ROWS * PACK], BF16)
-            codes = sb(name + "_codes", [P, ROWS], U32)
-            plane = sb(name + "_plane", [P, ROWS], U8)
-            nc.scalar.copy(
-                out=grouped[:].rearrange("p (a g b k) -> p g a k b", a=PAIRS, b=2, k=PACK),
-                in_=raw[:].rearrange("p k (g a b) -> p g a k b", a=PAIRS, b=2),
-            )
+        def quantise(name, raw, grouped, cut, code_slot, plane_slot):
+            codes = sb(name + "_codes", [P, ROWS], U32, tag=code_slot)
+            plane = sb(name + "_plane", [P, ROWS], U8, tag=plane_slot)
+            dst = grouped[:].rearrange("p (u j g k) -> p u g j k", u=2, j=4, k=PACK)
+            src = raw[:].rearrange("p k (g u j) -> p u g j k", u=2, j=4)
+            nc.scalar.copy(out=dst[:, :, :cut], in_=src[:, :, :cut])
+            if cut < TEAMS:
+                nc.vector.tensor_copy(out=dst[:, :, cut:], in_=src[:, :, cut:])
             nc.vector.quantize_mx(out=codes[:].bitcast(FP8X4), scales=plane[:], in_=grouped[:])
             return codes, plane
 
-        def products(names, words, plane, codes, code_plane):
-            banks = [psum.tile([P, 2, ROWS], F32, name=n, tag=n) for n in names]
-            for t in range(TILES):
-                cols = slice(t * P, (t + 1) * P)
-                nc.tensor.matmul_mx(
-                    out=banks[t // 2][:, t % 2, :],
-                    lhsT=words[:, cols].bitcast(FP4X4),
-                    lhsT_scale=plane[:, cols],
-                    rhs=codes[:].bitcast(FP8X4),
-                    rhs_scale=code_plane[:],
-                    start=True,
-                    stop=True,
-                )
-            return banks
-
-        offsets = keep.tile([P, SLOTS // 16], U16, name="offsets")
-        nc.sync.dma_start(offsets[:], offs)
-
-        key_plane = sb("key_plane", [P, POOL], U8)
-        val_plane = sb("val_plane", [P, POOL], U8)
-        nc.gpsimd.memset(key_plane[:].bitcast(I32), 0)
-        nc.vector.memset(val_plane[:].bitcast(I32), 0)
-
-        q_raw = sb("q_raw", [P, PACK, ROWS], F32)
-        key_words = sb("key_words", [P, POOL], U16)
-        val_words = sb("val_words", [P, POOL], U16)
-        us_sb = sb("us_sb", [P, TILES], F32)
-        res_sb = sb("res_sb", [P, TILES], F32)
-
-        nc.sync.dma_start(out=q_raw[:], in_=query.rearrange("(p k) q -> p k q", k=PACK))
-        load_scales(nc.sync, key_plane, keys_scales)
-        nc.sync.dma_start(out=key_words[:].bitcast(I32), in_=keys_words[0].bitcast(I32))
-        load_scales(nc.sync, val_plane, vals_scales)
-        nc.sync.dma_start(out=val_words[:].bitcast(I32), in_=vals_words[0].bitcast(I32))
-        with nc.allow_non_contiguous_dma(reason="one float32 for each slot"):
-            nc.gpsimd.dma_start(out=res_sb[:], in_=reserve.rearrange("(t p) o -> p (t o)", p=P))
-            nc.gpsimd.dma_start(out=us_sb[:], in_=us.rearrange("(t p) o -> p (t o)", p=P))
-
-        ident = sb("ident", [P, P], F32)
-        make_identity(nc, ident[:])
-        kappa = sb("kappa", [P, TILES], F32)
-        res_wide = sb("res_wide", [P, TILES, TEAMS], F32)
-
-        got_kplane = sb("got_kplane", [P, SLOTS], U8)
-        got_kwords = sb("got_kwords", [P, SLOTS], U16)
-        got_vplane = sb("got_vplane", [P, SLOTS], U8)
-        got_vwords = sb("got_vwords", [P, SLOTS], U16)
-
-        nc.vector.tensor_copy(got_kplane[:], key_plane[:].indirect(offsets[:]))
-        q_codes, q_plane = quantise("q", q_raw)
-        g_raw = sb("g_raw", [P, PACK, ROWS], F32, tag="q_raw")
-        nc.sync.dma_start(out=g_raw[:], in_=gout.rearrange("(p k) q -> p k q", k=PACK))
-        nc.scalar.mul(kappa[:], us_sb[:], math.sqrt(512.0))
-        nc.gpsimd.tensor_copy(out=res_wide[:], in_=res_sb[:].unsqueeze(2).to_broadcast([P, TILES, TEAMS]))
-        for h in range(2):
-            nc.vector.tensor_copy(got_kwords[:, h * 256 : (h + 1) * 256], key_words[:].indirect(offsets[:, h * 16 : (h + 1) * 16]))
-        base_sb = sb("base_sb", [P, TILES, ROWS], F32, tag="key_words")
-        nc.sync.dma_start(out=base_sb[:], in_=base.rearrange("(t p) q -> p t q", p=P))
-        a_banks = products(["bank0", "bank1"], got_kwords, got_kplane, q_codes, q_plane)
-
-        p_all = sb("p_all", [P, PAIRS, TILES * 2 * TEAMS], F32)
-        for t in range(TILES):
-            nc.scalar.activation(
-                out=p_all[:, :, t * 64 : (t + 1) * 64],
-                in_=a_banks[t // 2][:, t % 2, :].rearrange("p (a c) -> p a c", a=PAIRS),
-                func=ACT.Exp,
+        def product(dst, t, words, plane, codes, code_plane, cols):
+            slots = slice(t * P, (t + 1) * P)
+            nc.tensor.matmul_mx(
+                out=dst,
+                lhsT=words[:, slots].bitcast(FP4X4),
+                lhsT_scale=plane[:, slots],
+                rhs=codes[:, cols].bitcast(FP8X4),
+                rhs_scale=code_plane[:, cols],
+                start=True,
+                stop=True,
             )
 
-        def team_sums(bank, src, first):
-            blocks = list(first) + [src[:, a, b : 2 * P : 2] for a in range(PAIRS) for b in range(2)]
+        def team_sums(bank, src, last):
+            blocks = [src[:, j, :] for j in range(MATES)] + list(last)
             for n, block in enumerate(blocks):
                 nc.tensor.matmul(bank[:], lhsT=block, rhs=ident[:], is_transpose=True, start=(n == 0), stop=(n == len(blocks) - 1))
 
+        key_plane = sb("key_plane", [P, POOL], U8)
+        val_plane = sb("val_plane", [P, POOL], U8)
+        nc.vector.memset(key_plane[:].bitcast(I32), 0)
+        nc.vector.memset(val_plane[:].bitcast(I32), 0)
+        rows = sb("rows", [P, P], F32)
+        nc.gpsimd.memset(rows[:], 0.0)
+        zeros = sb("zeros", [P, P], F32, tag="val_words")
+        nc.gpsimd.memset(zeros[:], 0.0)
+        ident = sb("ident", [P, P], F32)
+        nc.gpsimd.affine_select(
+            out=ident[:], in_=zeros[:], compare_op=ALU.not_equal, fill=1.0, base=0, pattern=[[-1, P]], channel_multiplier=1
+        )
+
+        q_raw = sb("q_raw", [P, PACK, ROWS], F32)
+        key_words = sb("key_words", [P, POOL], U16)
+        offsets = keep.tile([P, SLOTS // 16], U16, name="offsets")
+
+        nc.sync.dma_start(offsets[:], offs)
+        nc.sync.dma_start(out=key_words[:].bitcast(I32), in_=keys_words[0].bitcast(I32))
+        nc.sync.dma_start(out=q_raw[:], in_=query.rearrange("(p k) q -> p k q", k=PACK))
+        nc.sync.dma_start(out=rows[0:TILES, :], in_=reserve.rearrange("(t p) o -> t (p o)", p=P))
+        nc.sync.dma_start(out=rows[TILES : 2 * TILES, :], in_=us.rearrange("(t p) o -> t (p o)", p=P))
+        load_scales(nc.sync, key_plane, keys_scales)
+        val_words = sb("val_words", [P, POOL], U16)
+        nc.sync.dma_start(out=val_words[:].bitcast(I32), in_=vals_words[0].bitcast(I32))
+        load_scales(nc.sync, val_plane, vals_scales)
+
+        cols_bank = psum.tile([P, P], F32, name="cols_bank", tag="bank6")
+        nc.tensor.transpose(cols_bank[:], rows[:], ident[:])
+
+        got_kplane = sb("got_kplane", [P, SLOTS], U8)
+        got_kwords = sb("got_kwords", [P, SLOTS], U16)
+
+        nc.vector.tensor_copy(got_kwords[:], key_words[:].indirect(offsets[:]))
+        g_raw = sb("g_raw", [P, PACK, ROWS], F32, tag="key_words")
+        nc.sync.dma_start(out=g_raw[:], in_=gout.rearrange("(p k) q -> p k q", k=PACK))
+        nc.vector.tensor_copy(got_kplane[:, 0:256], key_plane[:].indirect(offsets[:, 0:16]))
+        q_bf = shared.tile([P, ROWS * PACK], BF16, name="q_bf", align_bytes=64, offset=0)
+        q_codes, q_plane = quantise("q", q_raw, q_bf, 16, None, None)
+        nc.vector.tensor_copy(got_kplane[:, 256:512], key_plane[:].indirect(offsets[:, 16:32]))
+        base_sb = sb("base_sb", [P, TILES, ROWS], F32, tag="key_plane")
+        nc.sync.dma_start(out=base_sb[:], in_=base.rearrange("(t p) q -> p t q", p=P))
+        spread = sb("spread", [P, P + TILES], F32, tag="q_raw")
+        res_wide = spread[:, 0:P]
+        kappa = spread[:, P : P + TILES]
+        nc.scalar.copy(out=res_wide.rearrange("p (t g) -> p t g", t=TILES), in_=cols_bank[:, 0:TILES].unsqueeze(2).to_broadcast([P, TILES, TEAMS]))
+        nc.scalar.mul(kappa, cols_bank[:, TILES : 2 * TILES], math.sqrt(512.0))
+
+        def products(name, first_bank, order, words, plane, codes, code_plane):
+            banks = [psum.tile([P, TILES, P], F32, name="%s%d" % (name, u), tag="bank%d" % (first_bank + u)) for u in range(2)]
+            for u, t in order:
+                product(banks[u][:, t, :], t, words, plane, codes, code_plane, slice(u * P, (u + 1) * P))
+            return banks
+
+        a_banks = products("a_bank", 0, [(u, 2 * h + i) for h in range(2) for u in range(2) for i in range(2)], got_kwords, got_kplane, q_codes, q_plane)
+        p_all = sb("p_all", [P, MATES, P], F32)
+        for u in range(2):
+            nc.scalar.activation(
+                out=p_all[:, 4 * u : 4 * u + 4, :].rearrange("p j (t g) -> p j t g", t=TILES),
+                in_=a_banks[u][:].rearrange("p t (j g) -> p j t g", j=4),
+                func=ACT.Exp,
+            )
         sum_bank = psum.tile([P, P], F32, name="sum_bank", tag="bank4")
-        team_sums(sum_bank, p_all, [res_wide[:].rearrange("p t g -> p (t g)")])
+        team_sums(sum_bank, p_all, [res_wide])
 
-        nc.vector.tensor_copy(got_vplane[:], val_plane[:].indirect(offsets[:]))
+        got_vwords = shared.tile([P, SLOTS], U16, name="got_vwords", align_bytes=64, offset=0)
+        got_vplane = shared.tile([P, SLOTS], U8, name="got_vplane", align_bytes=64, offset=2 * SLOTS)
         nc.vector.tensor_copy(got_vwords[:], val_words[:].indirect(offsets[:]))
-        g_codes, g_plane = quantise("g", g_raw)
-        c_banks = products(["bank2", "bank3"], got_vwords, got_vplane, g_codes, g_plane)
+        nc.vector.tensor_copy(got_vplane[:], val_plane[:].indirect(offsets[:]))
+        g_bf = sb("g_bf", [P, ROWS * PACK], BF16)
+        g_codes, g_plane = quantise("g", g_raw, g_bf, 12, "val_plane", "val_words")
+        c_banks = products("c_bank", 2, [(u, t) for u in range(2) for t in range(TILES)], got_vwords, got_vplane, g_codes, g_plane)
 
-        inv_turned = sb("inv_turned", [P, P], F32)
+        inv_turned = sb("inv_turned", [P, P], F32, tag="g_bf")
         nc.vector.reciprocal(inv_turned[:], sum_bank[:])
         inv_bank = psum.tile([P, P], F32, name="inv_bank", tag="bank5")
         nc.tensor.transpose(inv_bank[:], inv_turned[:], ident[:])
 
-        s = [sb("s%d" % t, [P, ROWS], F32) for t in range(TILES)]
-        cs = [sb("cs%d" % t, [P, ROWS], F32) for t in range(TILES)]
-        m = [sb("m%d" % t, [P, TEAMS], F32) for t in range(TILES)]
-        x = [sb("x%d" % t, [P, ROWS], F32) for t in range(TILES)]
-        z = [sb("z%d" % t, [P, ROWS], F32) for t in range(TILES)]
+        cp = sb("cp", [P, MATES, P], F32)
+        for j in range(0, MATES, 2):
+            nc.vector.tensor_tensor(
+                out=cp[:, j : j + 2, :].rearrange("p j (t g) -> p j t g", t=TILES),
+                in0=c_banks[j // 4][:, :, (j % 4) * TEAMS : (j % 4 + 2) * TEAMS].rearrange("p t (j g) -> p j t g", j=2),
+                in1=p_all[:, j : j + 2, :].rearrange("p j (t g) -> p j t g", t=TILES),
+                op=ALU.mult,
+            )
+        cp_bank = psum.tile([P, P], F32, name="cp_bank", tag="bank6")
+        team_sums(cp_bank, cp, [])
+
+        s = [sb("s%d" % h, [P, MATES, 64], F32) for h in range(2)]
+
+        def shares(h):
+            nc.vector.tensor_tensor(
+                out=s[h][:], in0=p_all[:, :, h * 64 : (h + 1) * 64], in1=by_team(inv_bank[:, h * 64 : (h + 1) * 64], MATES), op=ALU.mult
+            )
+
+        shares(0)
+        mean_turned = sb("mean_turned", [P, P], F32)
+        nc.vector.tensor_tensor(out=mean_turned[:], in0=cp_bank[:], in1=inv_turned[:], op=ALU.mult)
+        mean_bank = psum.tile([P, P], F32, name="mean_bank", tag="bank7")
+        nc.tensor.transpose(mean_bank[:], mean_turned[:], ident[:])
+        mean = sb("mean", [P, P], F32)
+        nc.scalar.copy(out=mean[:], in_=mean_bank[:])
+        shares(1)
+
+        z = [sb("z%d" % h, [P, MATES, 64], F32) for h in range(2)]
         hw_banks = []
         for h in range(2):
-            tiles = (2 * h, 2 * h + 1)
-            terms = sb("terms%d" % h, [P, PAIRS, 2 * P], F32)
-            for t in tiles:
+            x = sb("x%d" % h, [P, MATES, 64], F32)
+            terms = sb("terms%d" % h, [P, MATES, P], F32)
+            for u in range(2):
                 nc.vector.tensor_tensor(
-                    out=dealt(s[t][:]),
-                    in0=p_all[:, :, t * 64 : (t + 1) * 64].rearrange("p a (g b) -> p a g b", b=2),
-                    in1=by_team(inv_bank[:, t * TEAMS : (t + 1) * TEAMS]),
-                    op=ALU.mult,
+                    out=x[:, 4 * u : 4 * u + 4, :].rearrange("p j (t g) -> p j t g", t=2),
+                    in0=c_banks[u][:, 2 * h : 2 * h + 2, :].rearrange("p t (j g) -> p j t g", j=4),
+                    in1=by_team(mean[:, h * 64 : (h + 1) * 64], 4).rearrange("p j (t g) -> p j t g", t=2),
+                    op=ALU.subtract,
                 )
-            for t in tiles:
-                nc.vector.tensor_tensor(out=cs[t][:], in0=c_banks[h][:, t % 2, :], in1=s[t][:], op=ALU.mult)
-            for t in tiles:
-                nc.vector.tensor_reduce(
-                    out=m[t][:], in_=cs[t][:].rearrange("p (a g b) -> p g a b", a=PAIRS, b=2), axis=AXIS.XY, op=ALU.add
-                )
-            for t in tiles:
-                nc.vector.tensor_tensor(out=dealt(x[t][:]), in0=dealt(c_banks[h][:, t % 2, :]), in1=by_team(m[t][:]), op=ALU.subtract)
-            for t in tiles:
+            for i in range(2):
+                cols = slice(i * TEAMS, (i + 1) * TEAMS)
                 nc.vector.scalar_tensor_tensor(
-                    out=z[t][:], in0=x[t][:], scalar=kappa[:, t : t + 1], in1=s[t][:], op0=ALU.mult, op1=ALU.mult
+                    out=z[h][:, :, cols], in0=x[:, :, cols], scalar=kappa[:, 2 * h + i : 2 * h + i + 1], in1=s[h][:, :, cols], op0=ALU.mult, op1=ALU.mult
                 )
-            for t in tiles:
-                at = (t % 2) * 64
-                nc.vector.tensor_tensor(
-                    out=terms[:, :, at : at + 64],
-                    in0=z[t][:].rearrange("p (a c) -> p a c", a=PAIRS),
-                    in1=s[t][:].rearrange("p (a c) -> p a c", a=PAIRS),
-                    op=ALU.mult,
-                )
-                nc.scalar.activation(
-                    out=terms[:, :, P + at : P + at + 64], in_=z[t][:].rearrange("p (a c) -> p a c", a=PAIRS), func=ACT.Square
-                )
-            turned_bank = psum.tile([P, P], F32, name="turned_bank%d" % h, tag=("bank6", "bank0")[h])
+            for i in range(2):
+                cols = slice(i * TEAMS, (i + 1) * TEAMS)
+                nc.vector.tensor_tensor(out=terms[:, :, cols], in0=z[h][:, :, cols], in1=s[h][:, :, cols], op=ALU.mult)
+                nc.scalar.activation(out=terms[:, :, 64 + i * TEAMS : 64 + (i + 1) * TEAMS], in_=z[h][:, :, cols], func=ACT.Square)
+            turned_bank = psum.tile([P, P], F32, name="turned_bank%d" % h, tag=("bank0", "bank4")[h])
             team_sums(turned_bank, terms, [])
             turned = sb("turned%d" % h, [P, P], F32)
             nc.scalar.copy(out=turned[:], in_=turned_bank[:])
-            hw_bank = psum.tile([P, P], F32, name="hw_bank%d" % h, tag=("bank7", "bank1")[h])
+            hw_bank = psum.tile([P, P], F32, name="hw_bank%d" % h, tag=("bank1", "bank6")[h])
             nc.tensor.transpose(hw_bank[:], turned[:], ident[:])
             hw_banks.append(hw_bank)
 
-        out_tiles = out.rearrange("(t p) q -> t p q", p=P)
-        for h in range(2):
-            tiles = (2 * h, 2 * h + 1)
-            zh = {t: sb("zh%d" % t, [P, ROWS], F32) for t in tiles}
-            ws = {t: sb("ws%d" % t, [P, ROWS], F32) for t in tiles}
-            zzh = {t: sb("zzh%d" % t, [P, ROWS], F32) for t in tiles}
-            ha = {t: sb("ha%d" % t, [P, ROWS], F32) for t in tiles}
-            for t in tiles:
-                at = (t % 2) * TEAMS
-                nc.vector.tensor_tensor(out=dealt(zh[t][:]), in0=dealt(z[t][:]), in1=by_team(hw_banks[h][:, at : at + TEAMS]), op=ALU.subtract)
-            for t in tiles:
-                at = (2 + t % 2) * TEAMS
-                nc.vector.tensor_tensor(out=dealt(ws[t][:]), in0=dealt(s[t][:]), in1=by_team(hw_banks[h][:, at : at + TEAMS]), op=ALU.mult)
-            for t in tiles:
-                nc.vector.tensor_tensor(out=zzh[t][:], in0=zh[t][:], in1=z[t][:], op=ALU.mult)
-            for t in tiles:
-                nc.vector.tensor_tensor(out=ha[t][:], in0=zzh[t][:], in1=ws[t][:], op=ALU.subtract)
-            for t in tiles:
-                res = sb("res%d" % t, [P, ROWS], F32)
-                nc.vector.tensor_tensor(
-                    out=res[:].rearrange("p (g a b) -> p g a b", a=PAIRS, b=2),
-                    in0=ha[t][:].rearrange("p (a g b) -> p g a b", a=PAIRS, b=2),
-                    in1=base_sb[:, t, :].rearrange("p (g a b) -> p g a b", a=PAIRS, b=2),
-                    op=ALU.add,
-                )
-                nc.sync.dma_start(out=out_tiles[t], in_=res[:])
+        out_tiles = out.rearrange("(t p) q -> p t q", p=P)
+        zh = [sb("zh%d" % h, [P, MATES, 64], F32) for h in range(2)]
+        ws = [sb("ws%d" % h, [P, MATES, 64], F32) for h in range(2)]
+        zzh = [sb("zzh%d" % h, [P, MATES, 64], F32) for h in range(2)]
+        ha = [sb("ha%d" % h, [P, MATES, 64], F32) for h in range(2)]
+
+        def centred(h):
+            nc.vector.tensor_tensor(out=zh[h][:], in0=z[h][:], in1=by_team(hw_banks[h][:, 0:64], MATES), op=ALU.subtract)
+
+        def weighted(h):
+            nc.vector.tensor_tensor(out=ws[h][:], in0=s[h][:], in1=by_team(hw_banks[h][:, 64:P], MATES), op=ALU.mult)
+
+        def squared(h, cols):
+            nc.vector.tensor_tensor(out=zzh[h][:, :, cols], in0=zh[h][:, :, cols], in1=z[h][:, :, cols], op=ALU.mult)
+
+        def joined(h, cols):
+            nc.vector.tensor_tensor(out=ha[h][:, :, cols], in0=zzh[h][:, :, cols], in1=ws[h][:, :, cols], op=ALU.subtract)
+
+        def finish(t0, count):
+            res = sb("res%d" % t0, [P, count, ROWS], F32)
+            at = (t0 % 2) * TEAMS
+            nc.vector.tensor_tensor(
+                out=res[:].rearrange("p t (g u j) -> p u (t g) j", u=2, j=4),
+                in0=ha[t0 // 2][:, :, at : at + TEAMS * count].rearrange("p (u j) g -> p u g j", u=2),
+                in1=base_sb[:, t0 : t0 + count, :].rearrange("p t (g u j) -> p u (t g) j", u=2, j=4),
+                op=ALU.add,
+            )
+            nc.sync.dma_start(out=out_tiles[:, t0 : t0 + count, :], in_=res[:])
+
+        whole, left, right = slice(0, 64), slice(0, TEAMS), slice(TEAMS, 64)
+        centred(0)
+        weighted(0)
+        squared(0, whole)
+        centred(1)
+        joined(0, whole)
+        weighted(1)
+        finish(0, 2)
+        squared(1, left)
+        squared(1, right)
+        joined(1, left)
+        joined(1, right)
+        finish(2, 1)
+        finish(3, 1)

@@ -157,6 +157,12 @@ def tile_attend_gpteamshares_kernel(tc, query, keys_words, keys_scales, reserve,
                 in1=p_all[:, j : j + 2, :].rearrange("p j (t g) -> p j t g", t=TILES),
                 op=ALU.mult,
             )
+        c_all = sb("c_all", [P, MATES, P], F32)
+        for u in range(2):
+            nc.scalar.copy(
+                out=c_all[:, 4 * u : 4 * u + 4, :].rearrange("p j (t g) -> p j t g", t=TILES),
+                in_=c_banks[u][:].rearrange("p t (j g) -> p j t g", j=4),
+            )
         cp_bank = psum.tile([P, P], F32, name="cp_bank", tag="bank6")
         team_sums(cp_bank, cp, [])
 
@@ -172,21 +178,18 @@ def tile_attend_gpteamshares_kernel(tc, query, keys_words, keys_scales, reserve,
         nc.vector.tensor_tensor(out=mean_turned[:], in0=cp_bank[:], in1=inv_turned[:], op=ALU.mult)
         mean_bank = psum.tile([P, P], F32, name="mean_bank", tag="bank7")
         nc.tensor.transpose(mean_bank[:], mean_turned[:], ident[:])
-        mean = sb("mean", [P, P], F32)
-        nc.scalar.copy(out=mean[:], in_=mean_bank[:])
         shares(1)
 
         z = [sb("z%d" % h, [P, MATES, 64], F32) for h in range(2)]
         hw_banks = []
+        start = []
         for h in range(2):
             x = sb("x%d" % h, [P, MATES, 64], F32)
             terms = sb("terms%d" % h, [P, MATES, P], F32)
-            for u in range(2):
+            for i in range(2):
+                teams = slice((2 * h + i) * TEAMS, (2 * h + i + 1) * TEAMS)
                 nc.vector.tensor_tensor(
-                    out=x[:, 4 * u : 4 * u + 4, :].rearrange("p j (t g) -> p j t g", t=2),
-                    in0=c_banks[u][:, 2 * h : 2 * h + 2, :].rearrange("p t (j g) -> p j t g", j=4),
-                    in1=by_team(mean[:, h * 64 : (h + 1) * 64], 4).rearrange("p j (t g) -> p j t g", t=2),
-                    op=ALU.subtract,
+                    out=x[:, :, i * TEAMS : (i + 1) * TEAMS], in0=c_all[:, :, teams], in1=by_team(mean_bank[:, teams], MATES), op=ALU.subtract
                 )
             for i in range(2):
                 cols = slice(i * TEAMS, (i + 1) * TEAMS)
@@ -204,47 +207,42 @@ def tile_attend_gpteamshares_kernel(tc, query, keys_words, keys_scales, reserve,
             hw_bank = psum.tile([P, P], F32, name="hw_bank%d" % h, tag=("bank1", "bank6")[h])
             nc.tensor.transpose(hw_bank[:], turned[:], ident[:])
             hw_banks.append(hw_bank)
+            start.append(sb("start%d" % h, [P, 2, ROWS], F32, tag="turned%d" % h))
+            nc.gpsimd.tensor_tensor(
+                out=start[h][:].rearrange("p t (g u j) -> p u (t g) j", u=2, j=4),
+                in0=terms[:, :, 64:P].rearrange("p (u j) g -> p u g j", u=2),
+                in1=base_sb[:, 2 * h : 2 * h + 2, :].rearrange("p t (g u j) -> p u (t g) j", u=2, j=4),
+                op=ALU.add,
+            )
 
         out_tiles = out.rearrange("(t p) q -> p t q", p=P)
-        zh = [sb("zh%d" % h, [P, MATES, 64], F32) for h in range(2)]
+        hz = [sb("hz%d" % h, [P, MATES, 64], F32) for h in range(2)]
         ws = [sb("ws%d" % h, [P, MATES, 64], F32) for h in range(2)]
-        zzh = [sb("zzh%d" % h, [P, MATES, 64], F32) for h in range(2)]
-        ha = [sb("ha%d" % h, [P, MATES, 64], F32) for h in range(2)]
-
-        def centred(h):
-            nc.vector.tensor_tensor(out=zh[h][:], in0=z[h][:], in1=by_team(hw_banks[h][:, 0:64], MATES), op=ALU.subtract)
+        minus = [sb("minus%d" % h, [P, MATES, 64], F32) for h in range(2)]
 
         def weighted(h):
+            nc.vector.tensor_tensor(out=hz[h][:], in0=z[h][:], in1=by_team(hw_banks[h][:, 0:64], MATES), op=ALU.mult)
             nc.vector.tensor_tensor(out=ws[h][:], in0=s[h][:], in1=by_team(hw_banks[h][:, 64:P], MATES), op=ALU.mult)
 
-        def squared(h, cols):
-            nc.vector.tensor_tensor(out=zzh[h][:, :, cols], in0=zh[h][:, :, cols], in1=z[h][:, :, cols], op=ALU.mult)
-
         def joined(h, cols):
-            nc.vector.tensor_tensor(out=ha[h][:, :, cols], in0=zzh[h][:, :, cols], in1=ws[h][:, :, cols], op=ALU.subtract)
+            nc.vector.tensor_tensor(out=minus[h][:, :, cols], in0=hz[h][:, :, cols], in1=ws[h][:, :, cols], op=ALU.add)
 
         def finish(t0, count):
             res = sb("res%d" % t0, [P, count, ROWS], F32)
-            at = (t0 % 2) * TEAMS
+            at = t0 % 2
             nc.vector.tensor_tensor(
                 out=res[:].rearrange("p t (g u j) -> p u (t g) j", u=2, j=4),
-                in0=ha[t0 // 2][:, :, at : at + TEAMS * count].rearrange("p (u j) g -> p u g j", u=2),
-                in1=base_sb[:, t0 : t0 + count, :].rearrange("p t (g u j) -> p u (t g) j", u=2, j=4),
-                op=ALU.add,
+                in0=start[t0 // 2][:, at : at + count, :].rearrange("p t (g u j) -> p u (t g) j", u=2, j=4),
+                in1=minus[t0 // 2][:, :, at * TEAMS : (at + count) * TEAMS].rearrange("p (u j) g -> p u g j", u=2),
+                op=ALU.subtract,
             )
             nc.sync.dma_start(out=out_tiles[:, t0 : t0 + count, :], in_=res[:])
 
-        whole, left, right = slice(0, 64), slice(0, TEAMS), slice(TEAMS, 64)
-        centred(0)
         weighted(0)
-        squared(0, whole)
-        centred(1)
-        joined(0, whole)
+        joined(0, slice(0, 64))
         weighted(1)
         finish(0, 2)
-        squared(1, left)
-        squared(1, right)
-        joined(1, left)
-        joined(1, right)
+        joined(1, slice(0, TEAMS))
+        joined(1, slice(TEAMS, 64))
         finish(2, 1)
         finish(3, 1)

import math
from contextlib import ExitStack

import concourse.mybir as mybir

F32 = mybir.dt.float32
BF16 = mybir.dt.bfloat16
I32 = mybir.dt.int32
U32 = mybir.dt.uint32
U16 = mybir.dt.uint16
U8 = mybir.dt.uint8
FP8X4 = mybir.dt.float8_e4m3fn_x4
FP4X4 = mybir.dt.float4_e2m1fn_x4
ALU = mybir.AluOpType
ACT = mybir.ActivationFunctionType
AXIS = mybir.AxisListType

P = 128
POOL = 2048
SLOTS = 512
ROWS = 256
TEAMS = 32
TILES = SLOTS // P
MATES = 8
PACK = 4
FLOPS = 2 * 2 * 512 * SLOTS * ROWS


def tile_attend_gpteamshares_kernel(tc, query, keys_words, keys_scales, reserve, us, gout, vals_words, vals_scales, base, offs, out):
    nc = tc.nc
    with ExitStack() as ctx:
        keep = ctx.enter_context(tc.tile_pool(name="keep", bufs=1))
        shared = ctx.enter_context(tc.tile_pool(name="shared", bufs=1))
        psum = ctx.enter_context(tc.psum_pool(name="psum", bufs=1))

        def sb(name, shape, dtype, tag=None):
            return keep.tile(shape, dtype, name=name, tag=tag or name, align_bytes=64)

        def load_scales(queue, plane, scales):
            for r in range(4):
                queue.dma_start(out=plane[r:P:32, :].bitcast(I32), in_=scales[0, r:16:4, :].bitcast(I32))

        def by_team(cols, mates):
            return cols.unsqueeze(1).to_broadcast([P, mates, cols.shape[1]])

        def quantise(name, raw, grouped, cut, code_slot, plane_slot):
            codes = sb(name + "_codes", [P, ROWS], U32, tag=code_slot)
            plane = sb(name + "_plane", [P, ROWS], U8, tag=plane_slot)
            dst = grouped[:].rearrange("p (u j g k) -> p u g j k", u=2, j=4, k=PACK)
            src = raw[:].rearrange("p k (g u j) -> p u g j k", u=2, j=4)
            nc.scalar.copy(out=dst[:, :, :cut], in_=src[:, :, :cut])
            if cut < TEAMS:
                nc.vector.tensor_copy(out=dst[:, :, cut:], in_=src[:, :, cut:])
            nc.vector.quantize_mx(out=codes[:].bitcast(FP8X4), scales=plane[:], in_=grouped[:])
            return codes, plane

        def product(dst, t, words, plane, codes, code_plane, cols):
            slots = slice(t * P, (t + 1) * P)
            nc.tensor.matmul_mx(
                out=dst,
                lhsT=words[:, slots].bitcast(FP4X4),
                lhsT_scale=plane[:, slots],
                rhs=codes[:, cols].bitcast(FP8X4),
                rhs_scale=code_plane[:, cols],
                start=True,
                stop=True,
            )

        def team_sums(bank, src, last):
            blocks = [src[:, j, :] for j in range(MATES)] + list(last)
            for n, block in enumerate(blocks):
                nc.tensor.matmul(bank[:], lhsT=block, rhs=ident[:], is_transpose=True, start=(n == 0), stop=(n == len(blocks) - 1))

        key_plane = sb("key_plane", [P, POOL], U8)
        val_plane = sb("val_plane", [P, POOL], U8)
        nc.vector.memset(key_plane[:].bitcast(I32), 0)
        nc.vector.memset(val_plane[:].bitcast(I32), 0)
        rows = sb("rows", [P, P], F32)
        nc.gpsimd.memset(rows[:], 0.0)
        zeros = sb("zeros", [P, P], F32, tag="val_words")
        nc.gpsimd.memset(zeros[:], 0.0)
        ident = sb("ident", [P, P], F32)
        nc.gpsimd.affine_select(
            out=ident[:], in_=zeros[:], compare_op=ALU.not_equal, fill=1.0, base=0, pattern=[[-1, P]], channel_multiplier=1
        )

        q_raw = sb("q_raw", [P, PACK, ROWS], F32)
        key_words = sb("key_words", [P, POOL], U16)
        offsets = keep.tile([P, SLOTS // 16], U16, name="offsets")

        nc.sync.dma_start(offsets[:], offs)
        nc.sync.dma_start(out=key_words[:].bitcast(I32), in_=keys_words[0].bitcast(I32))
        nc.sync.dma_start(out=q_raw[:], in_=query.rearrange("(p k) q -> p k q", k=PACK))
        nc.sync.dma_start(out=rows[0:TILES, :], in_=reserve.rearrange("(t p) o -> t (p o)", p=P))
        nc.sync.dma_start(out=rows[TILES : 2 * TILES, :], in_=us.rearrange("(t p) o -> t (p o)", p=P))
        load_scales(nc.sync, key_plane, keys_scales)
        val_words = sb("val_words", [P, POOL], U16)
        nc.sync.dma_start(out=val_words[:].bitcast(I32), in_=vals_words[0].bitcast(I32))
        load_scales(nc.sync, val_plane, vals_scales)

        cols_bank = psum.tile([P, P], F32, name="cols_bank", tag="bank6")
        nc.tensor.transpose(cols_bank[:], rows[:], ident[:])

        got_kplane = sb("got_kplane", [P, SLOTS], U8)
        got_kwords = sb("got_kwords", [P, SLOTS], U16)

        nc.vector.tensor_copy(got_kwords[:], key_words[:].indirect(offsets[:]))
        g_raw = sb("g_raw", [P, PACK, ROWS], F32, tag="key_words")
        nc.sync.dma_start(out=g_raw[:], in_=gout.rearrange("(p k) q -> p k q", k=PACK))
        nc.vector.tensor_copy(got_kplane[:, 0:256], key_plane[:].indirect(offsets[:, 0:16]))
        q_bf = shared.tile([P, ROWS * PACK], BF16, name="q_bf", align_bytes=64, offset=0)
        q_codes, q_plane = quantise("q", q_raw, q_bf, 16, None, None)
        nc.vector.tensor_copy(got_kplane[:, 256:512], key_plane[:].indirect(offsets[:, 16:32]))
        base_sb = sb("base_sb", [P, TILES, ROWS], F32, tag="key_plane")
        nc.sync.dma_start(out=base_sb[:], in_=base.rearrange("(t p) q -> p t q", p=P))
        spread = sb("spread", [P, P + TILES], F32, tag="q_raw")
        res_wide = spread[:, 0:P]
        kappa = spread[:, P : P + TILES]
        nc.scalar.copy(out=res_wide.rearrange("p (t g) -> p t g", t=TILES), in_=cols_bank[:, 0:TILES].unsqueeze(2).to_broadcast([P, TILES, TEAMS]))
        nc.scalar.mul(kappa, cols_bank[:, TILES : 2 * TILES], math.sqrt(512.0))

        def products(name, first_bank, order, words, plane, codes, code_plane):
            banks = [psum.tile([P, TILES, P], F32, name="%s%d" % (name, u), tag="bank%d" % (first_bank + u)) for u in range(2)]
            for u, t in order:
                product(banks[u][:, t, :], t, words, plane, codes, code_plane, slice(u * P, (u + 1) * P))
            return banks

        a_banks = products("a_bank", 0, [(u, 2 * h + i) for h in range(2) for u in range(2) for i in range(2)], got_kwords, got_kplane, q_codes, q_plane)
        p_all = sb("p_all", [P, MATES, P], F32)
        for u in range(2):
            nc.scalar.activation(
                out=p_all[:, 4 * u : 4 * u + 4, :].rearrange("p j (t g) -> p j t g", t=TILES),
                in_=a_banks[u][:].rearrange("p t (j g) -> p j t g", j=4),
                func=ACT.Exp,
            )
        sum_bank = psum.tile([P, P], F32, name="sum_bank", tag="bank4")
        team_sums(sum_bank, p_all, [res_wide])

        got_vwords = shared.tile([P, SLOTS], U16, name="got_vwords", align_bytes=64, offset=0)
        got_vplane = shared.tile([P, SLOTS], U8, name="got_vplane", align_bytes=64, offset=2 * SLOTS)
        nc.vector.tensor_copy(got_vwords[:], val_words[:].indirect(offsets[:]))
        nc.vector.tensor_copy(got_vplane[:], val_plane[:].indirect(offsets[:]))
        g_bf = sb("g_bf", [P, ROWS * PACK], BF16)
        g_codes, g_plane = quantise("g", g_raw, g_bf, 12, "val_plane", "val_words")
        c_banks = products("c_bank", 2, [(u, t) for u in range(2) for t in range(TILES)], got_vwords, got_vplane, g_codes, g_plane)

        inv_turned = sb("inv_turned", [P, P], F32, tag="g_bf")
        nc.vector.reciprocal(inv_turned[:], sum_bank[:])
        inv_bank = psum.tile([P, P], F32, name="inv_bank", tag="bank5")
        nc.tensor.transpose(inv_bank[:], inv_turned[:], ident[:])

        cp = sb("cp", [P, MATES, P], F32)
        for j in range(0, MATES, 2):
            nc.vector.tensor_tensor(
                out=cp[:, j : j + 2, :].rearrange("p j (t g) -> p j t g", t=TILES),
                in0=c_banks[j // 4][:, :, (j % 4) * TEAMS : (j % 4 + 2) * TEAMS].rearrange("p t (j g) -> p j t g", j=2),
                in1=p_all[:, j : j + 2, :].rearrange("p j (t g) -> p j t g", t=TILES),
                op=ALU.mult,
            )
        c_all = sb("c_all", [P, MATES, P], F32)
        for u in range(2):
            nc.scalar.copy(
                out=c_all[:, 4 * u : 4 * u + 4, :].rearrange("p j (t g) -> p j t g", t=TILES),
                in_=c_banks[u][:].rearrange("p t (j g) -> p j t g", j=4),
            )
        cp_bank = psum.tile([P, P], F32, name="cp_bank", tag="bank6")
        team_sums(cp_bank, cp, [])

        s = [sb("s%d" % h, [P, MATES, 64], F32) for h in range(2)]

        def shares(h):
            nc.vector.tensor_tensor(
                out=s[h][:], in0=p_all[:, :, h * 64 : (h + 1) * 64], in1=by_team(inv_bank[:, h * 64 : (h + 1) * 64], MATES), op=ALU.mult
            )

        shares(0)
        mean_turned = sb("mean_turned", [P, P], F32)
        nc.vector.tensor_tensor(out=mean_turned[:], in0=cp_bank[:], in1=inv_turned[:], op=ALU.mult)
        mean_bank = psum.tile([P, P], F32, name="mean_bank", tag="bank7")
        nc.tensor.transpose(mean_bank[:], mean_turned[:], ident[:])
        shares(1)

        z = [sb("z%d" % h, [P, MATES, 64], F32) for h in range(2)]
        hw_banks = []
        start = []
        for h in range(2):
            x = sb("x%d" % h, [P, MATES, 64], F32)
            terms = sb("terms%d" % h, [P, MATES, P], F32)
            for i in range(2):
                teams = slice((2 * h + i) * TEAMS, (2 * h + i + 1) * TEAMS)
                nc.vector.tensor_tensor(
                    out=x[:, :, i * TEAMS : (i + 1) * TEAMS], in0=c_all[:, :, teams], in1=by_team(mean_bank[:, teams], MATES), op=ALU.subtract
                )
            for i in range(2):
                cols = slice(i * TEAMS, (i + 1) * TEAMS)
                nc.vector.scalar_tensor_tensor(
                    out=z[h][:, :, cols], in0=x[:, :, cols], scalar=kappa[:, 2 * h + i : 2 * h + i + 1], in1=s[h][:, :, cols], op0=ALU.mult, op1=ALU.mult
                )
            for i in range(2):
                cols = slice(i * TEAMS, (i + 1) * TEAMS)
                nc.vector.tensor_tensor(out=terms[:, :, cols], in0=z[h][:, :, cols], in1=s[h][:, :, cols], op=ALU.mult)
                nc.scalar.activation(out=terms[:, :, 64 + i * TEAMS : 64 + (i + 1) * TEAMS], in_=z[h][:, :, cols], func=ACT.Square)
            turned_bank = psum.tile([P, P], F32, name="turned_bank%d" % h, tag=("bank0", "bank4")[h])
            team_sums(turned_bank, terms, [])
            turned = sb("turned%d" % h, [P, P], F32)
            nc.scalar.copy(out=turned[:], in_=turned_bank[:])
            hw_bank = psum.tile([P, P], F32, name="hw_bank%d" % h, tag=("bank1", "bank6")[h])
            nc.tensor.transpose(hw_bank[:], turned[:], ident[:])
            hw_banks.append(hw_bank)
            start.append(sb("start%d" % h, [P, 2, ROWS], F32, tag="turned%d" % h))
            nc.gpsimd.tensor_tensor(
                out=start[h][:].rearrange("p t (g u j) -> p u (t g) j", u=2, j=4),
                in0=terms[:, :, 64:P].rearrange("p (u j) g -> p u g j", u=2),
                in1=base_sb[:, 2 * h : 2 * h + 2, :].rearrange("p t (g u j) -> p u (t g) j", u=2, j=4),
                op=ALU.add,
            )

        out_tiles = out.rearrange("(t p) q -> p t q", p=P)
        hz = [sb("hz%d" % h, [P, MATES, 64], F32) for h in range(2)]
        ws = [sb("ws%d" % h, [P, MATES, 64], F32) for h in range(2)]
        minus = [sb("minus%d" % h, [P, MATES, 64], F32) for h in range(2)]

        def weighted(h):
            nc.vector.tensor_tensor(out=hz[h][:], in0=z[h][:], in1=by_team(hw_banks[h][:, 0:64], MATES), op=ALU.mult)
            nc.vector.tensor_tensor(out=ws[h][:], in0=s[h][:], in1=by_team(hw_banks[h][:, 64:P], MATES), op=ALU.mult)

        def joined(h, cols):
            nc.vector.tensor_tensor(out=minus[h][:, :, cols], in0=hz[h][:, :, cols], in1=ws[h][:, :, cols], op=ALU.add)

        def finish(t0, count):
            res = sb("res%d" % t0, [P, count, ROWS], F32)
            at = t0 % 2
            nc.vector.tensor_tensor(
                out=res[:].rearrange("p t (g u j) -> p u (t g) j", u=2, j=4),
                in0=start[t0 // 2][:, at : at + count, :].rearrange("p t (g u j) -> p u (t g) j", u=2, j=4),
                in1=minus[t0 // 2][:, :, at * TEAMS : (at + count) * TEAMS].rearrange("p (u j) g -> p u g j", u=2),
                op=ALU.subtract,
            )
            nc.sync.dma_start(out=out_tiles[:, t0 : t0 + count, :], in_=res[:])

        weighted(0)
        joined(0, slice(0, 64))
        weighted(1)
        finish(0, 2)
        joined(1, slice(0, TEAMS))
        joined(1, slice(TEAMS, 64))
        finish(2, 1)
        finish(3, 1)
